import numpy as np
import ml_dtypes


def mxq(x, axis, fmt="e4m3"):
    dtype, down = {"e4m3": (ml_dtypes.float8_e4m3fn, 7), "e5m2": (ml_dtypes.float8_e5m2, 14)}[fmt]
    v = np.moveaxis(np.asarray(x, np.float32).astype(ml_dtypes.bfloat16).astype(np.float64), axis, -1)
    blocks = v.reshape(v.shape[:-1] + (-1, 32))
    amax = np.abs(blocks).max(-1, keepdims=True)
    byte = np.maximum(np.where(amax > 0, np.frexp(amax)[1] - 1 + 127, 0) - down, 1)
    scale = np.exp2(byte - 127.0)
    codes = (blocks / scale).astype(np.float32).astype(dtype).astype(np.float64)
    return np.moveaxis((codes * scale).reshape(v.shape), -1, axis)


WIDE = False


def mx_kscale(k, group=512):
    if not WIDE:
        return np.ones(k)
    levels = np.array([18, -18])
    if group != 512:
        return np.exp2(np.random.permutation(np.resize(levels, k // group))).repeat(group)
    if k % 512:
        return np.exp2(np.random.permutation(np.resize(levels, k // 32))).repeat(32)
    a = np.empty((k // 512, 16))
    for p in range(k // 512):
        a[p, :8] = np.random.permutation(np.resize(levels, 8))
        for g in range(8):
            far = levels[np.abs(levels - a[p, g]) >= 10]
            a[p, g + 8] = far[np.random.randint(len(far))]
    return np.exp2(a.ravel()).repeat(32)


def f64(x):
    return np.asarray(x).astype(np.float64)


def sigmoid(v):
    return 1.0 / (1.0 + np.exp(-v))


G, D, M, N = 4, 128, 128, 512


def setup_inputs():
    n = np.random.standard_normal
    s_d = mx_kscale(D, 0)
    return {
        "h": (n((G, D, N)) * s_d[:, None]).astype(np.float32),
        "wi": (n((G, D, M)) / np.sqrt(D) / s_d[:, None]).astype(np.float32),
        "wf": (n((G, D, M)) / np.sqrt(D) / s_d[:, None]).astype(np.float32),
        "wo": (n((G, D, M)) / np.sqrt(D) / s_d[:, None]).astype(np.float32),
        "wc": (n((G, D, M)) / np.sqrt(D) / s_d[:, None]).astype(np.float32),
        "xi": (n((G, M, N))).astype(np.float32),
        "xf": (n((G, M, N))).astype(np.float32),
        "xo": (n((G, M, N))).astype(np.float32),
        "xc": (n((G, M, N))).astype(np.float32),
        "c": (n((G, M, N))).astype(np.float32),
    }


def reference(h, wi, wf, wo, wc, xi, xf, xo, xc, c):
    wiq = mxq(f64(wi), 1, "e4m3")
    hq = mxq(f64(h), 1, "e4m3")
    zi = wiq.transpose(0, 2, 1) @ hq
    wfq = mxq(f64(wf), 1, "e4m3")
    zf = wfq.transpose(0, 2, 1) @ hq
    woq = mxq(f64(wo), 1, "e4m3")
    zo = woq.transpose(0, 2, 1) @ hq
    wcq = mxq(f64(wc), 1, "e4m3")
    zc = wcq.transpose(0, 2, 1) @ hq
    cn = sigmoid(zf + f64(xf)) * f64(c) + sigmoid(zi + f64(xi)) * np.tanh(zc + f64(xc))
    y = sigmoid(zo + f64(xo)) * np.tanh(cn)
    return y

@@ -1,0 +1,282 @@
+from contextlib import ExitStack
+
+import concourse.mybir as mybir
+
+G, D, M, N = 4, 128, 128, 512
+FLOPS = 2 * 4 * G * D * M * N
+
+F32 = mybir.dt.float32
+BF16 = mybir.dt.bfloat16
+U32 = mybir.dt.uint32
+U8 = mybir.dt.uint8
+FP8X4 = mybir.dt.float8_e4m3fn_x4
+ACT = mybir.ActivationFunctionType
+ALU = mybir.AluOpType
+
+P = 128
+PACK = 4
+ROWS = D // PACK
+
+SCHEDULE = [
+    ("warm"),
+    ("ld_h",0),
+    ("ld_h",1),
+    ("ld_w","i"),
+    ("ld_w","c"),
+    ("ld_w","f"),
+    ("ld_x","i",3,0,512),
+    ("ld_x","i",0,0,512),
+    ("ld_x","c",0,0,512),
+    ("cast_h","V",0,0,160),
+    ("cast_h","A",0,160,256),
+    ("ld_x","i",1,0,512),
+    ("q_h",0),
+    ("cast_h","A",1,160,256),
+    ("ld_x","c",3,0,512),
+    ("cast_h","V",1,0,160),
+    ("cast_w","V","i",0,80),
+    ("cast_w","A","i",80,128),
+    ("ld_x","i",2,0,512),
+    ("q_h",1),
+    ("q_w","i"),
+    ("cast_w","A","c",0,80),
+    ("ld_x","f",3,0,512),
+    ("cast_w","V","c",80,128),
+    ("mm","i",3),
+    ("mm","i",0),
+    ("mm","i",1),
+    ("cast_w","V","f",0,80),
+    ("cast_w","A","f",80,128),
+    ("ld_x","f",0,0,512),
+    ("q_w","c"),
+    ("q_w","f"),
+    ("ld_x","c",1,0,512),
+    ("mm","c",0),
+    ("add","i",3,0,512),
+    ("ld_c",3,0,512),
+    ("add","i",0,0,512),
+    ("mm","f",3),
+    ("mm","i",2),
+    ("mm","c",3),
+    ("mm","c",1),
+    ("ld_x","f",2,0,512),
+    ("add","c",0,0,512),
+    ("act","i",0,0,512),
+    ("mm","f",0),
+    ("add","i",1,0,512),
+    ("ld_w","o"),
+    ("act","c",0,0,512),
+    ("add","c",3,0,512),
+    ("ld_x","c",2,0,512),
+    ("act","i",3,0,512),
+    ("mm","f",1),
+    ("mm","c",2),
+    ("add","i",2,0,512),
+    ("ld_x","o",2,0,512),
+    ("act","c",3,0,512),
+    ("mul1","V",1,0,0,512),
+    ("ld_c",0,0,512),
+    ("act","i",1,0,512),
+    ("mm","f",2),
+    ("add","f",3,0,512),
+    ("ld_x","o",0,0,512),
+    ("mul1","V",1,3,0,512),
+    ("ld_x","f",1,0,512),
+    ("act","f",3,0,512),
+    ("add","c",1,0,512),
+    ("ld_x","o",3,0,512),
+    ("add","f",0,0,512),
+    ("act","c",1,0,512),
+    ("ld_c",1,0,512),
+    ("mul1","V",0,3,0,512),
+    ("cast_w","A","o",0,128),
+    ("ld_c",2,0,512),
+    ("add","f",2,0,512),
+    ("ld_x","o",1,0,512),
+    ("act","f",0,0,512),
+    ("add","c",2,0,512),
+    ("act","f",2,0,512),
+    ("cell","V",3,0,512),
+    ("act","c",2,0,512),
+    ("q_w","o"),
+    ("mul1","V",1,1,0,512),
+    ("mm","o",2),
+    ("mm","o",0),
+    ("act","i",2,0,512),
+    ("mm","o",3),
+    ("mm","o",1),
+    ("mul1","V",0,0,0,512),
+    ("tanh",3,0,512),
+    ("add","f",1,0,512),
+    ("add","o",0,0,512),
+    ("act","f",1,0,512),
+    ("add","o",3,0,512),
+    ("add","o",2,0,512),
+    ("act","o",3,0,512),
+    ("cell","V",0,0,512),
+    ("mul1","V",0,2,0,512),
+    ("tanh",0,0,512),
+    ("mul1","V",0,1,0,512),
+    ("act","o",2,0,512),
+    ("mul1","V",1,2,0,512),
+    ("act","o",0,0,512),
+    ("cell","V",1,0,512),
+    ("add","o",1,0,512),
+    ("tanh",1,0,512),
+    ("fin","V",3,0,256),
+    ("act","o",1,0,512),
+    ("cell","V",2,0,512),
+    ("st",3,0,256),
+    ("fin","V",3,256,512),
+    ("tanh",2,0,512),
+    ("fin","V",0,0,512),
+    ("st",3,256,512),
+    ("fin","V",1,0,512),
+    ("st",0,0,512),
+    ("fin","V",2,0,512),
+    ("st",1,0,512),
+    ("st",2,0,512),
+]
+
+
+def tile_rows_cell_lstm_kernel(tc, h, wi, wf, wo, wc, xi, xf, xo, xc, c, out):
+    nc = tc.nc
+    w_hbm = {"i": wi, "f": wf, "o": wo, "c": wc}
+    x_hbm = {"i": xi, "f": xf, "o": xo, "c": xc}
+    with ExitStack() as ctx:
+        sb = ctx.enter_context(tc.tile_pool(name="sb", bufs=1))
+        ps = ctx.enter_context(tc.psum_pool(name="ps", bufs=1))
+        eng = {"V": nc.vector, "G": nc.gpsimd}
+
+        HP = 2
+        HW = N // HP
+        h_raw = [sb.tile([P, PACK, HW], F32, name="h_raw%d" % q) for q in range(HP)]
+        h_bf = [sb.tile([P, HW, PACK], BF16, name="h_bf%d" % q, align_bytes=64) for q in range(HP)]
+        h_codes = sb.tile([P, N], U32, name="h_codes", align_bytes=64)
+        h_scales = sb.tile([P, N], U8, name="h_scales", align_bytes=64)
+        w_raw, w_bf, w_codes, w_scales = {}, {}, {}, {}
+        for k in "fico":
+            w_raw[k] = sb.tile([P, PACK, M], F32, name="w_raw_" + k)
+            w_bf[k] = sb.tile([P, M, PACK], BF16, name="w_bf_" + k, align_bytes=64)
+            w_codes[k] = sb.tile([P, M], U32, name="w_codes_" + k, align_bytes=64)
+            w_scales[k] = sb.tile([P, M], U8, name="w_scales_" + k, align_bytes=64)
+        x_sb, pre = {}, {}
+        for g in range(G):
+            for k in "fico":
+                x_sb[k, g] = sb.tile([P, N], F32, name="x_%s%d" % (k, g))
+                pre[k, g] = sb.tile([P, N], F32, name="pre_%s%d" % (k, g))
+        gates = [sb.tile([P, 2, N], F32, name="gates%d" % g) for g in range(G)]
+        vals = [sb.tile([P, 2, N], F32, name="vals%d" % g) for g in range(G)]
+        prod = [sb.tile([P, 2, N], F32, name="prod%d" % g) for g in range(G)]
+        ogate = [sb.tile([P, N], F32, name="ogate%d" % g) for g in range(G)]
+        cell = [sb.tile([P, N], F32, name="cell%d" % g) for g in range(G)]
+        tcell = [sb.tile([P, N], F32, name="tcell%d" % g) for g in range(G)]
+        res = [sb.tile([P, N], F32, name="res%d" % g) for g in range(G)]
+        banks = [[ps.tile([P, N], F32, name="z%d_%d" % (g, b)) for b in range(2)] for g in range(G)]
+        bank_of = {"i":0,"c":1,"f":0,"o":1}
+        warm_in = sb.tile([P, 8], F32, name="warm_in")
+        warm_out = sb.tile([P, 8], F32, name="warm_out")
+
+        def act_dst(k, g):
+            if k == "f":
+                return gates[g][:, 0, :]
+            if k == "i":
+                return gates[g][:, 1, :]
+            if k == "c":
+                return vals[g][:, 1, :]
+            return ogate[g][:]
+
+        ctx.enter_context(tc.manual_schedule())
+        for step in SCHEDULE:
+            op = step[0]
+            if op == "warm":
+                nc.vector.memset(warm_in[:], 0.0)
+                nc.scalar.activation(out=warm_out[:], in_=warm_in[:], func=ACT.Sigmoid)
+            elif op == "ld_h":
+                q = step[1]
+                nc.sync.dma_start(
+                    out=h_raw[q][:],
+                    in_=h.rearrange("g (p j) n -> (g p) j n", j=PACK)[:, :, q * HW : (q + 1) * HW],
+                )
+            elif op == "ld_w":
+                k = step[1]
+                nc.sync.dma_start(out=w_raw[k][:], in_=w_hbm[k].rearrange("g (p j) m -> (g p) j m", j=PACK))
+            elif op == "ld_x":
+                k, g, a, b = step[1:]
+                nc.sync.dma_start(out=x_sb[k, g][:, a:b], in_=x_hbm[k][g, :, a:b])
+            elif op == "ld_c":
+                g, a, b = step[1:]
+                nc.sync.dma_start(out=vals[g][:, 0, a:b], in_=c[g, :, a:b])
+            elif op == "cast_h" or op == "cast_w":
+                e, k, a, b = step[1:]
+                if op == "cast_h":
+                    dst, src = h_bf[k][:, a:b, :], h_raw[k][:, :, a:b].rearrange("p j n -> p n j")
+                else:
+                    dst, src = w_bf[k][:, a:b, :], w_raw[k][:, :, a:b].rearrange("p j n -> p n j")
+                if e == "A":
+                    nc.scalar.copy(out=dst, in_=src)
+                elif e == "V":
+                    nc.vector.tensor_copy(out=dst, in_=src)
+                else:
+                    nc.gpsimd.tensor_scalar(out=dst, in0=src, scalar1=1.0, scalar2=0.0, op0=ALU.mult, op1=ALU.add)
+            elif op == "q_h":
+                q = step[1]
+                cols = slice(q * HW, (q + 1) * HW)
+                nc.vector.quantize_mx(
+                    out=h_codes[:, cols].bitcast(FP8X4),
+                    scales=h_scales[:, cols],
+                    in_=h_bf[q][:].rearrange("p n j -> p (n j)"),
+                )
+            elif op == "q_w":
+                k = step[1]
+                nc.vector.quantize_mx(
+                    out=w_codes[k][:].bitcast(FP8X4),
+                    scales=w_scales[k][:],
+                    in_=w_bf[k][:].rearrange("p m j -> p (m j)"),
+                )
+            elif op == "mm":
+                k, g = step[1:]
+                rows = slice(ROWS * g, ROWS * (g + 1))
+                nc.tensor.matmul_mx(
+                    out=banks[g][bank_of[k]][:],
+                    lhsT=w_codes[k][rows, :].bitcast(FP8X4),
+                    lhsT_scale=w_scales[k][rows, :],
+                    rhs=h_codes[rows, :].bitcast(FP8X4),
+                    rhs_scale=h_scales[rows, :],
+                    start=True,
+                    stop=True,
+                )
+            elif op == "add":
+                k, g, a, b = step[1:]
+                nc.vector.tensor_tensor(
+                    out=pre[k, g][:, a:b], in0=banks[g][bank_of[k]][:, a:b], in1=x_sb[k, g][:, a:b], op=ALU.add
+                )
+            elif op == "act":
+                k, g, a, b = step[1:]
+                nc.scalar.activation(
+                    out=act_dst(k, g)[:, a:b],
+                    in_=pre[k, g][:, a:b],
+                    func=ACT.Tanh if k == "c" else ACT.Sigmoid,
+                )
+            elif op == "mul2":
+                e, g, a, b = step[1:]
+                eng[e].tensor_tensor(
+                    out=prod[g][:, :, a:b], in0=gates[g][:, :, a:b], in1=vals[g][:, :, a:b], op=ALU.mult
+                )
+            elif op == "mul1":
+                e, s, g, a, b = step[1:]
+                eng[e].tensor_tensor(
+                    out=prod[g][:, s, a:b], in0=gates[g][:, s, a:b], in1=vals[g][:, s, a:b], op=ALU.mult
+                )
+            elif op == "cell":
+                e, g, a, b = step[1:]
+                eng[e].tensor_tensor(out=cell[g][:, a:b], in0=prod[g][:, 0, a:b], in1=prod[g][:, 1, a:b], op=ALU.add)
+            elif op == "tanh":
+                g, a, b = step[1:]
+                nc.scalar.activation(out=tcell[g][:, a:b], in_=cell[g][:, a:b], func=ACT.Tanh)
+            elif op == "fin":
+                e, g, a, b = step[1:]
+                eng[e].tensor_tensor(out=res[g][:, a:b], in0=ogate[g][:, a:b], in1=tcell[g][:, a:b], op=ALU.mult)
+            elif op == "st":
+                g, a, b = step[1:]
+                nc.sync.dma_start(out=out[g, :, a:b], in_=res[g][:, a:b])

@@ -20,122 +20,118 @@ ROWS = D // PACK
 SCHEDULE = [
     ("warm"),
     ("ld_h",0),
+    ("ld_w","c"),
     ("ld_h",1),
     ("ld_w","i"),
-    ("ld_w","c"),
     ("ld_w","f"),
-    ("ld_x","i",3,0,512),
-    ("ld_x","i",0,0,512),
-    ("ld_x","c",0,0,512),
+    ("ld_w","o"),
+    ("ld_x","c",2,0,512),
+    ("ld_x","i",2,0,512),
     ("cast_h","V",0,0,160),
     ("cast_h","A",0,160,256),
     ("ld_x","i",1,0,512),
+    ("cast_w","A","c",0,128),
+    ("ld_x","c",1,0,512),
     ("q_h",0),
+    ("q_w","c"),
     ("cast_h","A",1,160,256),
-    ("ld_x","c",3,0,512),
+    ("ld_x","i",0,0,512),
     ("cast_h","V",1,0,160),
-    ("cast_w","V","i",0,80),
-    ("cast_w","A","i",80,128),
-    ("ld_x","i",2,0,512),
+    ("cast_w","V","i",80,128),
+    ("cast_w","A","i",0,80),
+    ("ld_x","c",0,0,512),
     ("q_h",1),
+    ("cast_w","A","f",0,128),
+    ("ld_x","f",1,0,512),
     ("q_w","i"),
-    ("cast_w","A","c",0,80),
-    ("ld_x","f",3,0,512),
-    ("cast_w","V","c",80,128),
+    ("mm","c",2),
+    ("mm","c",1),
+    ("cast_w","V","o",0,128),
+    ("ld_x","f",0,0,512),
     ("mm","i",3),
+    ("mm","i",2),
+    ("mm","c",0),
     ("mm","i",0),
     ("mm","i",1),
-    ("cast_w","V","f",0,80),
-    ("cast_w","A","f",80,128),
-    ("ld_x","f",0,0,512),
-    ("q_w","c"),
     ("q_w","f"),
-    ("ld_x","c",1,0,512),
-    ("mm","c",0),
-    ("add","i",3,0,512),
-    ("ld_c",3,0,512),
+    ("ld_x","i",3,0,512),
+    ("q_w","o"),
+    ("add","c",2,0,512),
+    ("ld_c",1,0,512),
+    ("add","i",2,0,512),
+    ("act","c",2,0,512),
+    ("mm","o",2),
+    ("ld_c",0,0,512),
+    ("add","i",1,0,512),
+    ("act","i",2,0,512),
+    ("ld_x","c",3,0,512),
+    ("add","c",1,0,512),
+    ("act","i",1,0,512),
+    ("mm","f",1),
     ("add","i",0,0,512),
-    ("mm","f",3),
-    ("mm","i",2),
-    ("mm","c",3),
-    ("mm","c",1),
-    ("ld_x","f",2,0,512),
+    ("ld_x","o",0,0,512),
+    ("mul1","G",1,2,0,512),
+    ("act","c",1,0,512),
+    ("mm","o",1),
     ("add","c",0,0,512),
+    ("ld_x","o",1,0,512),
     ("act","i",0,0,512),
     ("mm","f",0),
-    ("add","i",1,0,512),
-    ("ld_w","o"),
-    ("act","c",0,0,512),
-    ("add","c",3,0,512),
-    ("ld_x","c",2,0,512),
-    ("act","i",3,0,512),
-    ("mm","f",1),
-    ("mm","c",2),
-    ("add","i",2,0,512),
-    ("ld_x","o",2,0,512),
-    ("act","c",3,0,512),
-    ("mul1","V",1,0,0,512),
-    ("ld_c",0,0,512),
-    ("act","i",1,0,512),
-    ("mm","f",2),
-    ("add","f",3,0,512),
-    ("ld_x","o",0,0,512),
-    ("mul1","V",1,3,0,512),
-    ("ld_x","f",1,0,512),
-    ("act","f",3,0,512),
-    ("add","c",1,0,512),
-    ("ld_x","o",3,0,512),
-    ("add","f",0,0,512),
-    ("act","c",1,0,512),
-    ("ld_c",1,0,512),
-    ("mul1","V",0,3,0,512),
-    ("cast_w","A","o",0,128),
-    ("ld_c",2,0,512),
-    ("add","f",2,0,512),
-    ("ld_x","o",1,0,512),
-    ("act","f",0,0,512),
-    ("add","c",2,0,512),
-    ("act","f",2,0,512),
-    ("cell","V",3,0,512),
-    ("act","c",2,0,512),
-    ("q_w","o"),
-    ("mul1","V",1,1,0,512),
-    ("mm","o",2),
-    ("mm","o",0),
-    ("act","i",2,0,512),
-    ("mm","o",3),
-    ("mm","o",1),
-    ("mul1","V",0,0,0,512),
-    ("tanh",3,0,512),
     ("add","f",1,0,512),
-    ("add","o",0,0,512),
+    ("ld_x","f",2,0,512),
+    ("mul1","G",1,1,0,512),
+    ("act","c",0,0,512),
+    ("mm","o",0),
+    ("mm","f",2),
+    ("add","f",0,0,512),
+    ("ld_x","o",2,0,512),
     ("act","f",1,0,512),
-    ("add","o",3,0,512),
-    ("add","o",2,0,512),
-    ("act","o",3,0,512),
-    ("cell","V",0,0,512),
-    ("mul1","V",0,2,0,512),
-    ("tanh",0,0,512),
+    ("add","i",3,0,512),
+    ("ld_x","f",3,0,512),
+    ("act","f",0,0,512),
+    ("mul1","V",1,0,0,512),
+    ("ld_x","o",3,0,512),
+    ("act","i",3,0,512),
+    ("mm","f",3),
+    ("mm","c",3),
     ("mul1","V",0,1,0,512),
-    ("act","o",2,0,512),
-    ("mul1","V",1,2,0,512),
-    ("act","o",0,0,512),
-    ("cell","V",1,0,512),
+    ("ld_c",2,0,512),
+    ("mul1","V",0,0,0,512),
+    ("ld_c",3,0,512),
+    ("add","c",3,0,512),
+    ("cell","G",1,0,512),
+    ("add","o",0,0,512),
+    ("act","c",3,0,512),
+    ("mm","o",3),
     ("add","o",1,0,512),
+    ("cell","G",0,0,512),
     ("tanh",1,0,512),
-    ("fin","V",3,0,256),
-    ("act","o",1,0,512),
-    ("cell","V",2,0,512),
-    ("st",3,0,256),
-    ("fin","V",3,256,512),
-    ("tanh",2,0,512),
+    ("add","f",2,0,512),
+    ("act","o",0,0,512),
+    ("add","o",2,0,512),
+    ("mul1","G",1,3,0,512),
+    ("tanh",0,0,512),
+    ("add","f",3,0,512),
+    ("act","f",2,0,512),
+    ("add","o",3,0,512),
+    ("act","f",3,0,512),
     ("fin","V",0,0,512),
-    ("st",3,256,512),
-    ("fin","V",1,0,512),
+    ("act","o",1,0,512),
+    ("mul1","V",0,2,0,512),
     ("st",0,0,512),
+    ("act","o",3,0,512),
+    ("mul1","V",0,3,0,512),
+    ("act","o",2,0,512),
+    ("cell","V",2,0,512),
+    ("cell","V",3,0,512),
+    ("tanh",2,0,512),
+    ("fin","V",1,0,512),
+    ("tanh",3,0,512),
     ("fin","V",2,0,512),
     ("st",1,0,512),
+    ("fin","V",3,0,512),
     ("st",2,0,512),
+    ("st",3,0,512),
 ]
 
 

@@ -16,263 +16,194 @@ ALU = mybir.AluOpType
 P = 128
 PACK = 4
 ROWS = D // PACK
+HALF = N // 2
+GATES = "cifo"
 
-SCHEDULE = [
-    ("warm"),
-    ("ld_h",0),
-    ("ld_w","c"),
-    ("ld_h",1),
-    ("ld_w","i"),
-    ("ld_w","f"),
-    ("ld_w","o"),
-    ("ld_x","c",2,0,512),
-    ("ld_x","i",2,0,512),
-    ("cast_h","V",0,0,160),
-    ("cast_h","A",0,160,256),
-    ("ld_x","i",1,0,512),
-    ("cast_w","A","c",0,128),
-    ("ld_x","c",1,0,512),
-    ("q_h",0),
-    ("q_w","c"),
-    ("cast_h","A",1,160,256),
-    ("ld_x","i",0,0,512),
-    ("cast_h","V",1,0,160),
-    ("cast_w","V","i",80,128),
-    ("cast_w","A","i",0,80),
-    ("ld_x","c",0,0,512),
-    ("q_h",1),
-    ("cast_w","A","f",0,128),
-    ("ld_x","f",1,0,512),
-    ("q_w","i"),
-    ("mm","c",2),
-    ("mm","c",1),
-    ("cast_w","V","o",0,128),
-    ("ld_x","f",0,0,512),
-    ("mm","i",3),
-    ("mm","i",2),
-    ("mm","c",0),
-    ("mm","i",0),
-    ("mm","i",1),
-    ("q_w","f"),
-    ("ld_x","i",3,0,512),
-    ("q_w","o"),
-    ("add","c",2,0,512),
-    ("ld_c",1,0,512),
-    ("add","i",2,0,512),
-    ("act","c",2,0,512),
-    ("mm","o",2),
-    ("ld_c",0,0,512),
-    ("add","i",1,0,512),
-    ("act","i",2,0,512),
-    ("ld_x","c",3,0,512),
-    ("add","c",1,0,512),
-    ("act","i",1,0,512),
-    ("mm","f",1),
-    ("add","i",0,0,512),
-    ("ld_x","o",0,0,512),
-    ("mul1","G",1,2,0,512),
-    ("act","c",1,0,512),
-    ("mm","o",1),
-    ("add","c",0,0,512),
-    ("ld_x","o",1,0,512),
-    ("act","i",0,0,512),
-    ("mm","f",0),
-    ("add","f",1,0,512),
-    ("ld_x","f",2,0,512),
-    ("mul1","G",1,1,0,512),
-    ("act","c",0,0,512),
-    ("mm","o",0),
-    ("mm","f",2),
-    ("add","f",0,0,512),
-    ("ld_x","o",2,0,512),
-    ("act","f",1,0,512),
-    ("add","i",3,0,512),
-    ("ld_x","f",3,0,512),
-    ("act","f",0,0,512),
-    ("mul1","V",1,0,0,512),
-    ("ld_x","o",3,0,512),
-    ("act","i",3,0,512),
-    ("mm","f",3),
-    ("mm","c",3),
-    ("mul1","V",0,1,0,512),
-    ("ld_c",2,0,512),
-    ("mul1","V",0,0,0,512),
-    ("ld_c",3,0,512),
-    ("add","c",3,0,512),
-    ("cell","G",1,0,512),
-    ("add","o",0,0,512),
-    ("act","c",3,0,512),
-    ("mm","o",3),
-    ("add","o",1,0,512),
-    ("cell","G",0,0,512),
-    ("tanh",1,0,512),
-    ("add","f",2,0,512),
-    ("act","o",0,0,512),
-    ("add","o",2,0,512),
-    ("mul1","G",1,3,0,512),
-    ("tanh",0,0,512),
-    ("add","f",3,0,512),
-    ("act","f",2,0,512),
-    ("add","o",3,0,512),
-    ("act","f",3,0,512),
-    ("fin","V",0,0,512),
-    ("act","o",1,0,512),
-    ("mul1","V",0,2,0,512),
-    ("st",0,0,512),
-    ("act","o",3,0,512),
-    ("mul1","V",0,3,0,512),
-    ("act","o",2,0,512),
-    ("cell","V",2,0,512),
-    ("cell","V",3,0,512),
-    ("tanh",2,0,512),
-    ("fin","V",1,0,512),
-    ("tanh",3,0,512),
-    ("fin","V",2,0,512),
-    ("st",1,0,512),
-    ("fin","V",3,0,512),
-    ("st",2,0,512),
-    ("st",3,0,512),
-]
+BANK_OF = {"c": 0, "f": 0, "i": 1, "o": 1}
+
+H_VECTOR_COLS = (192, 176)
+WI_VECTOR_COLS = 80
 
 
 def tile_rows_cell_lstm_kernel(tc, h, wi, wf, wo, wc, xi, xf, xo, xc, c, out):
     nc = tc.nc
-    w_hbm = {"i": wi, "f": wf, "o": wo, "c": wc}
-    x_hbm = {"i": xi, "f": xf, "o": xo, "c": xc}
+    w_hbm = {"c": wc, "i": wi, "f": wf, "o": wo}
+    x_hbm = {"c": xc, "i": xi, "f": xf, "o": xo}
+
     with ExitStack() as ctx:
-        sb = ctx.enter_context(tc.tile_pool(name="sb", bufs=1))
-        ps = ctx.enter_context(tc.psum_pool(name="ps", bufs=1))
-        eng = {"V": nc.vector, "G": nc.gpsimd}
+        sbuf = ctx.enter_context(tc.tile_pool(name="sbuf", bufs=1))
+        psum = ctx.enter_context(tc.psum_pool(name="psum", bufs=1))
 
-        HP = 2
-        HW = N // HP
-        h_raw = [sb.tile([P, PACK, HW], F32, name="h_raw%d" % q) for q in range(HP)]
-        h_bf = [sb.tile([P, HW, PACK], BF16, name="h_bf%d" % q, align_bytes=64) for q in range(HP)]
-        h_codes = sb.tile([P, N], U32, name="h_codes", align_bytes=64)
-        h_scales = sb.tile([P, N], U8, name="h_scales", align_bytes=64)
-        w_raw, w_bf, w_codes, w_scales = {}, {}, {}, {}
-        for k in "fico":
-            w_raw[k] = sb.tile([P, PACK, M], F32, name="w_raw_" + k)
-            w_bf[k] = sb.tile([P, M, PACK], BF16, name="w_bf_" + k, align_bytes=64)
-            w_codes[k] = sb.tile([P, M], U32, name="w_codes_" + k, align_bytes=64)
-            w_scales[k] = sb.tile([P, M], U8, name="w_scales_" + k, align_bytes=64)
-        x_sb, pre = {}, {}
-        for g in range(G):
-            for k in "fico":
-                x_sb[k, g] = sb.tile([P, N], F32, name="x_%s%d" % (k, g))
-                pre[k, g] = sb.tile([P, N], F32, name="pre_%s%d" % (k, g))
-        gates = [sb.tile([P, 2, N], F32, name="gates%d" % g) for g in range(G)]
-        vals = [sb.tile([P, 2, N], F32, name="vals%d" % g) for g in range(G)]
-        prod = [sb.tile([P, 2, N], F32, name="prod%d" % g) for g in range(G)]
-        ogate = [sb.tile([P, N], F32, name="ogate%d" % g) for g in range(G)]
-        cell = [sb.tile([P, N], F32, name="cell%d" % g) for g in range(G)]
-        tcell = [sb.tile([P, N], F32, name="tcell%d" % g) for g in range(G)]
-        res = [sb.tile([P, N], F32, name="res%d" % g) for g in range(G)]
-        banks = [[ps.tile([P, N], F32, name="z%d_%d" % (g, b)) for b in range(2)] for g in range(G)]
-        bank_of = {"i":0,"c":1,"f":0,"o":1}
-        warm_in = sb.tile([P, 8], F32, name="warm_in")
-        warm_out = sb.tile([P, 8], F32, name="warm_out")
+        h_raw = [sbuf.tile([P, PACK, HALF], F32, name="h_raw%d" % q) for q in range(2)]
+        h_bf16 = [sbuf.tile([P, HALF, PACK], BF16, name="h_bf16_%d" % q, align_bytes=64) for q in range(2)]
+        h_codes = sbuf.tile([P, N], U32, name="h_codes", align_bytes=64)
+        h_scales = sbuf.tile([P, N], U8, name="h_scales", align_bytes=64)
+        w_raw = {k: sbuf.tile([P, PACK, M], F32, name="w_raw_" + k) for k in GATES}
+        w_bf16 = {k: sbuf.tile([P, M, PACK], BF16, name="w_bf16_" + k, align_bytes=64) for k in GATES}
+        w_codes = {k: sbuf.tile([P, M], U32, name="w_codes_" + k, align_bytes=64) for k in GATES}
+        w_scales = {k: sbuf.tile([P, M], U8, name="w_scales_" + k, align_bytes=64) for k in GATES}
 
-        def act_dst(k, g):
-            if k == "f":
-                return gates[g][:, 0, :]
-            if k == "i":
-                return gates[g][:, 1, :]
-            if k == "c":
-                return vals[g][:, 1, :]
-            return ogate[g][:]
+        x_sb = {k: sbuf.tile([P, G, N], F32, name="x_" + k) for k in GATES}
+        pre = {k: sbuf.tile([P, G, N], F32, name="pre_" + k) for k in GATES}
+        gate = {k: sbuf.tile([P, G, N], F32, name="gate_" + k) for k in GATES}
+        cell_old = sbuf.tile([P, G, N], F32, name="cell_old")
+        kept = sbuf.tile([P, G, N], F32, name="kept")
+        fresh = sbuf.tile([P, G, N], F32, name="fresh")
+        cell_new = sbuf.tile([P, G, N], F32, name="cell_new")
+        cell_tanh = sbuf.tile([P, G, N], F32, name="cell_tanh")
+        result = sbuf.tile([P, G, N], F32, name="result")
+        warm_in = sbuf.tile([P, 8], F32, name="warm_in")
+        warm_out = sbuf.tile([P, 8], F32, name="warm_out")
 
+        banks = [[psum.tile([P, N], F32, name="z%d_%d" % (g, b)) for b in range(2)] for g in range(G)]
+
+        def load_features(dst, src):
+            nc.sync.dma_start(out=dst[:], in_=src.rearrange("g (p j) n -> (g p) j n", j=PACK))
+
+        def load_h(q):
+            nc.sync.dma_start(
+                out=h_raw[q][:],
+                in_=h.rearrange("g (p j) n -> (g p) j n", j=PACK)[:, :, q * HALF : (q + 1) * HALF],
+            )
+
+        def load_heads(dst, src, first, last):
+            if first == last:
+                nc.sync.dma_start(out=dst[:, first, :], in_=src[first])
+            else:
+                both = slice(first, last + 1, last - first)
+                nc.sync.dma_start(out=dst[:, both, :], in_=src.rearrange("g m n -> m g n")[:, both, :])
+
+        def round_to_bf16(dst, raw, vector_cols):
+            width = raw.shape[2]
+            if vector_cols > 0:
+                nc.vector.tensor_copy(
+                    out=dst[:, :vector_cols, :], in_=raw[:, :, :vector_cols].rearrange("p j n -> p n j")
+                )
+            if vector_cols < width:
+                nc.scalar.copy(out=dst[:, vector_cols:, :], in_=raw[:, :, vector_cols:].rearrange("p j n -> p n j"))
+
+        def quantise(codes, scales, values):
+            nc.vector.quantize_mx(
+                out=codes.bitcast(FP8X4), scales=scales, in_=values[:].rearrange("p n j -> p (n j)")
+            )
+
+        def quantise_h(q):
+            cols = slice(q * HALF, (q + 1) * HALF)
+            quantise(h_codes[:, cols], h_scales[:, cols], h_bf16[q])
+
+        def quantise_w(k):
+            quantise(w_codes[k][:], w_scales[k][:], w_bf16[k])
+
+        def make_gate(k, g):
+            rows = slice(ROWS * g, ROWS * (g + 1))
+            z = banks[g][BANK_OF[k]]
+            nc.tensor.matmul_mx(
+                out=z[:],
+                lhsT=w_codes[k][rows, :].bitcast(FP8X4),
+                lhsT_scale=w_scales[k][rows, :],
+                rhs=h_codes[rows, :].bitcast(FP8X4),
+                rhs_scale=h_scales[rows, :],
+                start=True,
+                stop=True,
+            )
+            nc.vector.tensor_tensor(out=pre[k][:, g, :], in0=z[:], in1=x_sb[k][:, g, :], op=ALU.add)
+            nc.scalar.activation(
+                out=gate[k][:, g, :], in_=pre[k][:, g, :], func=ACT.Tanh if k == "c" else ACT.Sigmoid
+            )
+
+        def make_fresh(engine, g):
+            engine.tensor_tensor(out=fresh[:, g, :], in0=gate["i"][:, g, :], in1=gate["c"][:, g, :], op=ALU.mult)
+
+        def make_kept(engine, g):
+            engine.tensor_tensor(out=kept[:, g, :], in0=gate["f"][:, g, :], in1=cell_old[:, g, :], op=ALU.mult)
+
+        def make_cell(engine, g):
+            engine.tensor_tensor(out=cell_new[:, g, :], in0=kept[:, g, :], in1=fresh[:, g, :], op=ALU.add)
+
+        def squash_cell(g):
+            nc.scalar.activation(out=cell_tanh[:, g, :], in_=cell_new[:, g, :], func=ACT.Tanh)
+
+        def finish(g):
+            nc.vector.tensor_tensor(
+                out=result[:, g, :], in0=gate["o"][:, g, :], in1=cell_tanh[:, g, :], op=ALU.mult
+            )
+            nc.sync.dma_start(out=out[g], in_=result[:, g, :])
+
+        vector, gpsimd = nc.vector, nc.gpsimd
         ctx.enter_context(tc.manual_schedule())
-        for step in SCHEDULE:
-            op = step[0]
-            if op == "warm":
-                nc.vector.memset(warm_in[:], 0.0)
-                nc.scalar.activation(out=warm_out[:], in_=warm_in[:], func=ACT.Sigmoid)
-            elif op == "ld_h":
-                q = step[1]
-                nc.sync.dma_start(
-                    out=h_raw[q][:],
-                    in_=h.rearrange("g (p j) n -> (g p) j n", j=PACK)[:, :, q * HW : (q + 1) * HW],
-                )
-            elif op == "ld_w":
-                k = step[1]
-                nc.sync.dma_start(out=w_raw[k][:], in_=w_hbm[k].rearrange("g (p j) m -> (g p) j m", j=PACK))
-            elif op == "ld_x":
-                k, g, a, b = step[1:]
-                nc.sync.dma_start(out=x_sb[k, g][:, a:b], in_=x_hbm[k][g, :, a:b])
-            elif op == "ld_c":
-                g, a, b = step[1:]
-                nc.sync.dma_start(out=vals[g][:, 0, a:b], in_=c[g, :, a:b])
-            elif op == "cast_h" or op == "cast_w":
-                e, k, a, b = step[1:]
-                if op == "cast_h":
-                    dst, src = h_bf[k][:, a:b, :], h_raw[k][:, :, a:b].rearrange("p j n -> p n j")
-                else:
-                    dst, src = w_bf[k][:, a:b, :], w_raw[k][:, :, a:b].rearrange("p j n -> p n j")
-                if e == "A":
-                    nc.scalar.copy(out=dst, in_=src)
-                elif e == "V":
-                    nc.vector.tensor_copy(out=dst, in_=src)
-                else:
-                    nc.gpsimd.tensor_scalar(out=dst, in0=src, scalar1=1.0, scalar2=0.0, op0=ALU.mult, op1=ALU.add)
-            elif op == "q_h":
-                q = step[1]
-                cols = slice(q * HW, (q + 1) * HW)
-                nc.vector.quantize_mx(
-                    out=h_codes[:, cols].bitcast(FP8X4),
-                    scales=h_scales[:, cols],
-                    in_=h_bf[q][:].rearrange("p n j -> p (n j)"),
-                )
-            elif op == "q_w":
-                k = step[1]
-                nc.vector.quantize_mx(
-                    out=w_codes[k][:].bitcast(FP8X4),
-                    scales=w_scales[k][:],
-                    in_=w_bf[k][:].rearrange("p m j -> p (m j)"),
-                )
-            elif op == "mm":
-                k, g = step[1:]
-                rows = slice(ROWS * g, ROWS * (g + 1))
-                nc.tensor.matmul_mx(
-                    out=banks[g][bank_of[k]][:],
-                    lhsT=w_codes[k][rows, :].bitcast(FP8X4),
-                    lhsT_scale=w_scales[k][rows, :],
-                    rhs=h_codes[rows, :].bitcast(FP8X4),
-                    rhs_scale=h_scales[rows, :],
-                    start=True,
-                    stop=True,
-                )
-            elif op == "add":
-                k, g, a, b = step[1:]
-                nc.vector.tensor_tensor(
-                    out=pre[k, g][:, a:b], in0=banks[g][bank_of[k]][:, a:b], in1=x_sb[k, g][:, a:b], op=ALU.add
-                )
-            elif op == "act":
-                k, g, a, b = step[1:]
-                nc.scalar.activation(
-                    out=act_dst(k, g)[:, a:b],
-                    in_=pre[k, g][:, a:b],
-                    func=ACT.Tanh if k == "c" else ACT.Sigmoid,
-                )
-            elif op == "mul2":
-                e, g, a, b = step[1:]
-                eng[e].tensor_tensor(
-                    out=prod[g][:, :, a:b], in0=gates[g][:, :, a:b], in1=vals[g][:, :, a:b], op=ALU.mult
-                )
-            elif op == "mul1":
-                e, s, g, a, b = step[1:]
-                eng[e].tensor_tensor(
-                    out=prod[g][:, s, a:b], in0=gates[g][:, s, a:b], in1=vals[g][:, s, a:b], op=ALU.mult
-                )
-            elif op == "cell":
-                e, g, a, b = step[1:]
-                eng[e].tensor_tensor(out=cell[g][:, a:b], in0=prod[g][:, 0, a:b], in1=prod[g][:, 1, a:b], op=ALU.add)
-            elif op == "tanh":
-                g, a, b = step[1:]
-                nc.scalar.activation(out=tcell[g][:, a:b], in_=cell[g][:, a:b], func=ACT.Tanh)
-            elif op == "fin":
-                e, g, a, b = step[1:]
-                eng[e].tensor_tensor(out=res[g][:, a:b], in0=ogate[g][:, a:b], in1=tcell[g][:, a:b], op=ALU.mult)
-            elif op == "st":
-                g, a, b = step[1:]
-                nc.sync.dma_start(out=out[g, :, a:b], in_=res[g][:, a:b])
+
+        nc.vector.memset(warm_in[:], 0.0)
+        nc.scalar.activation(out=warm_out[:], in_=warm_in[:], func=ACT.Sigmoid)
+
+        load_h(0)
+        load_h(1)
+        for k in "cif":
+            load_features(w_raw[k], w_hbm[k])
+        for k, first, last in (("c", 0, 0), ("i", 0, 0), ("c", 1, 1), ("i", 1, 2), ("c", 2, 2)):
+            load_heads(x_sb[k], x_hbm[k], first, last)
+        for g in range(3):
+            load_heads(x_sb["f"], xf, g, g)
+        load_heads(cell_old, c, 0, 1)
+        load_features(w_raw["o"], wo)
+        load_heads(x_sb["c"], xc, 3, 3)
+        load_heads(x_sb["i"], xi, 3, 3)
+        load_heads(cell_old, c, 2, 2)
+        load_heads(x_sb["f"], xf, 3, 3)
+        load_heads(x_sb["o"], xo, 0, 3)
+        load_heads(cell_old, c, 3, 3)
+        load_heads(x_sb["o"], xo, 1, 1)
+        load_heads(x_sb["o"], xo, 2, 2)
+
+        round_to_bf16(h_bf16[0], h_raw[0], H_VECTOR_COLS[0])
+        quantise_h(0)
+        round_to_bf16(h_bf16[1], h_raw[1], H_VECTOR_COLS[1])
+        round_to_bf16(w_bf16["c"], w_raw["c"], M)
+        quantise_h(1)
+        quantise_w("c")
+        round_to_bf16(w_bf16["i"], w_raw["i"], WI_VECTOR_COLS)
+        quantise_w("i")
+        round_to_bf16(w_bf16["f"], w_raw["f"], 0)
+
+        make_gate("c", 0)
+        quantise_w("f")
+        make_gate("i", 0)
+        make_fresh(gpsimd, 0)
+        make_gate("c", 1)
+        make_gate("i", 1)
+        make_fresh(gpsimd, 1)
+        make_gate("c", 2)
+        make_gate("i", 2)
+        for g in range(3):
+            make_gate("f", g)
+
+        make_fresh(vector, 2)
+        make_kept(vector, 0)
+        make_kept(vector, 1)
+        round_to_bf16(w_bf16["o"], w_raw["o"], 0)
+
+        make_cell(gpsimd, 0)
+        make_gate("c", 3)
+        make_gate("i", 3)
+        squash_cell(0)
+
+        quantise_w("o")
+        make_kept(vector, 2)
+        make_cell(vector, 1)
+        squash_cell(1)
+
+        make_cell(gpsimd, 2)
+        make_gate("f", 3)
+        make_gate("o", 0)
+        squash_cell(2)
+
+        make_fresh(vector, 3)
+
+        make_kept(gpsimd, 3)
+        for g in (3, 1, 2):
+            make_gate("o", g)
+
+        finish(0)
+        make_cell(vector, 3)
+        squash_cell(3)
+        for g in (1, 2, 3):
+            finish(g)

from contextlib import ExitStack

import concourse.mybir as mybir

G, D, M, N = 4, 128, 128, 512
FLOPS = 2 * 4 * G * D * M * N

F32 = mybir.dt.float32
BF16 = mybir.dt.bfloat16
U32 = mybir.dt.uint32
U8 = mybir.dt.uint8
FP8X4 = mybir.dt.float8_e4m3fn_x4
ACT = mybir.ActivationFunctionType
ALU = mybir.AluOpType

P = 128
PACK = 4
ROWS = D // PACK
HALF = N // 2
GATES = "cifo"

BANK_OF = {"c": 0, "f": 0, "i": 1, "o": 1}

H_VECTOR_COLS = (192, 176)
WI_VECTOR_COLS = 80


def tile_rows_cell_lstm_kernel(tc, h, wi, wf, wo, wc, xi, xf, xo, xc, c, out):
    nc = tc.nc
    w_hbm = {"c": wc, "i": wi, "f": wf, "o": wo}
    x_hbm = {"c": xc, "i": xi, "f": xf, "o": xo}

    with ExitStack() as ctx:
        sbuf = ctx.enter_context(tc.tile_pool(name="sbuf", bufs=1))
        psum = ctx.enter_context(tc.psum_pool(name="psum", bufs=1))

        h_raw = [sbuf.tile([P, PACK, HALF], F32, name="h_raw%d" % q) for q in range(2)]
        h_bf16 = [sbuf.tile([P, HALF, PACK], BF16, name="h_bf16_%d" % q, align_bytes=64) for q in range(2)]
        h_codes = sbuf.tile([P, N], U32, name="h_codes", align_bytes=64)
        h_scales = sbuf.tile([P, N], U8, name="h_scales", align_bytes=64)
        w_raw = {k: sbuf.tile([P, PACK, M], F32, name="w_raw_" + k) for k in GATES}
        w_bf16 = {k: sbuf.tile([P, M, PACK], BF16, name="w_bf16_" + k, align_bytes=64) for k in GATES}
        w_codes = {k: sbuf.tile([P, M], U32, name="w_codes_" + k, align_bytes=64) for k in GATES}
        w_scales = {k: sbuf.tile([P, M], U8, name="w_scales_" + k, align_bytes=64) for k in GATES}

        x_sb = {k: sbuf.tile([P, G, N], F32, name="x_" + k) for k in GATES}
        pre = {k: sbuf.tile([P, G, N], F32, name="pre_" + k) for k in GATES}
        gate = {k: sbuf.tile([P, G, N], F32, name="gate_" + k) for k in GATES}
        cell_old = sbuf.tile([P, G, N], F32, name="cell_old")
        kept = sbuf.tile([P, G, N], F32, name="kept")
        fresh = sbuf.tile([P, G, N], F32, name="fresh")
        cell_new = sbuf.tile([P, G, N], F32, name="cell_new")
        cell_tanh = sbuf.tile([P, G, N], F32, name="cell_tanh")
        result = sbuf.tile([P, G, N], F32, name="result")
        warm_in = sbuf.tile([P, 8], F32, name="warm_in")
        warm_out = sbuf.tile([P, 8], F32, name="warm_out")

        banks = [[psum.tile([P, N], F32, name="z%d_%d" % (g, b)) for b in range(2)] for g in range(G)]

        def load_features(dst, src):
            nc.sync.dma_start(out=dst[:], in_=src.rearrange("g (p j) n -> (g p) j n", j=PACK))

        def load_h(q):
            nc.sync.dma_start(
                out=h_raw[q][:],
                in_=h.rearrange("g (p j) n -> (g p) j n", j=PACK)[:, :, q * HALF : (q + 1) * HALF],
            )

        def load_heads(dst, src, first, last):
            if first == last:
                nc.sync.dma_start(out=dst[:, first, :], in_=src[first])
            else:
                both = slice(first, last + 1, last - first)
                nc.sync.dma_start(out=dst[:, both, :], in_=src.rearrange("g m n -> m g n")[:, both, :])

        def round_to_bf16(dst, raw, vector_cols):
            width = raw.shape[2]
            if vector_cols > 0:
                nc.vector.tensor_copy(
                    out=dst[:, :vector_cols, :], in_=raw[:, :, :vector_cols].rearrange("p j n -> p n j")
                )
            if vector_cols < width:
                nc.scalar.copy(out=dst[:, vector_cols:, :], in_=raw[:, :, vector_cols:].rearrange("p j n -> p n j"))

        def quantise(codes, scales, values):
            nc.vector.quantize_mx(
                out=codes.bitcast(FP8X4), scales=scales, in_=values[:].rearrange("p n j -> p (n j)")
            )

        def quantise_h(q):
            cols = slice(q * HALF, (q + 1) * HALF)
            quantise(h_codes[:, cols], h_scales[:, cols], h_bf16[q])

        def quantise_w(k):
            quantise(w_codes[k][:], w_scales[k][:], w_bf16[k])

        def make_gate(k, g):
            rows = slice(ROWS * g, ROWS * (g + 1))
            z = banks[g][BANK_OF[k]]
            nc.tensor.matmul_mx(
                out=z[:],
                lhsT=w_codes[k][rows, :].bitcast(FP8X4),
                lhsT_scale=w_scales[k][rows, :],
                rhs=h_codes[rows, :].bitcast(FP8X4),
                rhs_scale=h_scales[rows, :],
                start=True,
                stop=True,
            )
            nc.vector.tensor_tensor(out=pre[k][:, g, :], in0=z[:], in1=x_sb[k][:, g, :], op=ALU.add)
            nc.scalar.activation(
                out=gate[k][:, g, :], in_=pre[k][:, g, :], func=ACT.Tanh if k == "c" else ACT.Sigmoid
            )

        def make_fresh(engine, g):
            engine.tensor_tensor(out=fresh[:, g, :], in0=gate["i"][:, g, :], in1=gate["c"][:, g, :], op=ALU.mult)

        def make_kept(engine, g):
            engine.tensor_tensor(out=kept[:, g, :], in0=gate["f"][:, g, :], in1=cell_old[:, g, :], op=ALU.mult)

        def make_cell(engine, g):
            engine.tensor_tensor(out=cell_new[:, g, :], in0=kept[:, g, :], in1=fresh[:, g, :], op=ALU.add)

        def squash_cell(g):
            nc.scalar.activation(out=cell_tanh[:, g, :], in_=cell_new[:, g, :], func=ACT.Tanh)

        def finish(g):
            nc.vector.tensor_tensor(
                out=result[:, g, :], in0=gate["o"][:, g, :], in1=cell_tanh[:, g, :], op=ALU.mult
            )
            nc.sync.dma_start(out=out[g], in_=result[:, g, :])

        vector, gpsimd = nc.vector, nc.gpsimd
        ctx.enter_context(tc.manual_schedule())

        nc.vector.memset(warm_in[:], 0.0)
        nc.scalar.activation(out=warm_out[:], in_=warm_in[:], func=ACT.Sigmoid)

        load_h(0)
        load_h(1)
        for k in "cif":
            load_features(w_raw[k], w_hbm[k])
        for k, first, last in (("c", 0, 0), ("i", 0, 0), ("c", 1, 1), ("i", 1, 2), ("c", 2, 2)):
            load_heads(x_sb[k], x_hbm[k], first, last)
        for g in range(3):
            load_heads(x_sb["f"], xf, g, g)
        load_heads(cell_old, c, 0, 1)
        load_features(w_raw["o"], wo)
        load_heads(x_sb["c"], xc, 3, 3)
        load_heads(x_sb["i"], xi, 3, 3)
        load_heads(cell_old, c, 2, 2)
        load_heads(x_sb["f"], xf, 3, 3)
        load_heads(x_sb["o"], xo, 0, 3)
        load_heads(cell_old, c, 3, 3)
        load_heads(x_sb["o"], xo, 1, 1)
        load_heads(x_sb["o"], xo, 2, 2)

        round_to_bf16(h_bf16[0], h_raw[0], H_VECTOR_COLS[0])
        quantise_h(0)
        round_to_bf16(h_bf16[1], h_raw[1], H_VECTOR_COLS[1])
        round_to_bf16(w_bf16["c"], w_raw["c"], M)
        quantise_h(1)
        quantise_w("c")
        round_to_bf16(w_bf16["i"], w_raw["i"], WI_VECTOR_COLS)
        quantise_w("i")
        round_to_bf16(w_bf16["f"], w_raw["f"], 0)

        make_gate("c", 0)
        quantise_w("f")
        make_gate("i", 0)
        make_fresh(gpsimd, 0)
        make_gate("c", 1)
        make_gate("i", 1)
        make_fresh(gpsimd, 1)
        make_gate("c", 2)
        make_gate("i", 2)
        for g in range(3):
            make_gate("f", g)

        make_fresh(vector, 2)
        make_kept(vector, 0)
        make_kept(vector, 1)
        round_to_bf16(w_bf16["o"], w_raw["o"], 0)

        make_cell(gpsimd, 0)
        make_gate("c", 3)
        make_gate("i", 3)
        squash_cell(0)

        quantise_w("o")
        make_kept(vector, 2)
        make_cell(vector, 1)
        squash_cell(1)

        make_cell(gpsimd, 2)
        make_gate("f", 3)
        make_gate("o", 0)
        squash_cell(2)

        make_fresh(vector, 3)

        make_kept(gpsimd, 3)
        for g in (3, 1, 2):
            make_gate("o", g)

        finish(0)
        make_cell(vector, 3)
        squash_cell(3)
        for g in (1, 2, 3):
            finish(g)
